import numpy as np
CORES = [3,7,11,15,131,135,139,143]
N = 8
R, T = 4096, 256
CAPP = 64
def entries(a): return a.T.reshape(-1)
def pack(v, P): return np.ascontiguousarray(np.asarray(v, np.int32).reshape(-1, P).T)
def lists(rng, how):
    I = rng.integers(0, N * R, (N, T))
    O = np.stack([rng.permutation(np.repeat(np.arange(N), CAPP))[:T] for r in range(N)])
    if how == "full": O = np.stack([rng.permutation(np.repeat(rng.permutation(N)[:T // CAPP], CAPP)) for r in range(N)])
    I = R * O + rng.integers(0, R, (N, T))
    if how == "alike": I = R * O + rng.integers(0, R, (N, 1))
    if how == "edge": I = R * O + np.where(rng.random((N, T)) < 0.5, 0, R - 1)
    if how == "sorted": I = np.sort(I, axis=1)
    return {"idx": np.stack([pack(I[r], 16) for r in range(N)])}
def setup_inputs(rng):
    return dict({"tab": rng.standard_normal((N, 128, R), dtype=np.float32)}, **lists(rng, "uniform"))
def setup_inputs_alike(rng):
    d = setup_inputs(rng); d.update(lists(rng, "alike"))
    for k in ("tab",): d[k] = (d[k].astype(np.float32) * 1048576.0).astype(d[k].dtype)
    return d
def setup_inputs_edge(rng):
    d = setup_inputs(rng); d.update(lists(rng, "edge"))
    for k in ("tab",): d[k] = (d[k].astype(np.float32) * (1 / 1024.0)).astype(d[k].dtype)
    return d
def setup_inputs_full(rng):
    d = setup_inputs(rng); d.update(lists(rng, "full"))
    return d
def setup_inputs_sorted(rng):
    d = setup_inputs(rng); d.update(lists(rng, "sorted"))
    return d
def check_inputs(x):
    bad = []
    if x["idx"].min() < 0 or x["idx"].max() >= N * R: bad.append("idx out of range")
    if max(int(np.bincount(entries(a) // R, minlength=N).max()) for a in x["idx"]) > CAPP: bad.append("more than CAPP entries of a list point into one rank's part")
    return bad
def reference(tab, idx):
    A = np.concatenate(list(tab), axis=1)
    return {"y": np.stack([A[:, entries(idx[r])] for r in range(N)])}

@@ -1,0 +1,209 @@
+from concourse.bass import DstId, RemoteDMATransfer
+from concourse.mybir import AluOpType, AxisListType
+
+N, R, L, CAP = 8, 4096, 256, 64
+BW = CAP // 16
+QW = N * BW
+
+SCRATCH = {
+    "tabs": ("sbuf", [128, R], "float32"),
+    "ent": ("sbuf", [128, 2], "int32"),
+    "oli": ("sbuf", [128, 4], "int32"),
+    "olf": ("sbuf", [128, 4], "float32"),
+    "eh": ("sbuf", [128, 24], "float32"),
+    "ones": ("sbuf", [128, 128], "float32"),
+    "upper": ("sbuf", [128, 128], "float32"),
+    "io16": ("sbuf", [128, 16], "float32"),
+    "m16": ("sbuf", [128, 128], "float32"),
+    "c32": ("sbuf", [128, QW], "float32"),
+    "prod": ("sbuf", [128, 16], "float32"),
+    "slotf": ("sbuf", [128, 2], "float32"),
+    "sloti": ("sbuf", [128, 2], "int32"),
+    "mdi": ("sbuf", [128, 4], "int32"),
+    "mdf": ("sbuf", [128, 4], "float32"),
+    "lq": ("sbuf", [128, 256], "float32"),
+    "rq": ("sbuf", [128, 2 * QW], "float32"),
+    "qall": ("sbuf", [128, N * QW], "uint16"),
+    "ai": ("sbuf", [128, 128], "int32"),
+    "af": ("sbuf", [128, 128], "float32"),
+    "bi": ("sbuf", [128, 32], "int32"),
+    "bf": ("sbuf", [128, 32], "float32"),
+    "lf": ("sbuf", [128, 256], "float32"),
+    "fin": ("sbuf", [128, 16], "uint16"),
+    "snd": ("sbuf", [128, N * CAP], "float32"),
+    "land": ("sbuf", [128, N * CAP], "float32"),
+    "ysb": ("sbuf", [128, L], "float32"),
+    "pc": ("psum", [128, 512], "float32"),
+    "pq": ("psum", [128, 512], "float32"),
+    "pf": ("psum", [128, 512], "float32"),
+}
+SEMAPHORES = ["ldi", "ldt", "cv", "ca", "cb", "cc", "vv", "vt", "tv", "qs", "gs0", "gs1", "gs2", "gs3", "done", "st",
+              "req", "dat", "loc"]
+
+
+def _bits(m):
+    return [b for b in range(m.bit_length()) if (m >> b) & 1]
+
+
+def _mask(engines):
+    return sum(1 << b for b in engines)
+
+
+def _plan(c, cores, topo):
+    peers = [d for d in cores if d != c]
+    near = [d for d in peers if topo.host(d) == topo.host(c) and topo.chip(d) == topo.chip(c)]
+    mate = [d for d in peers if topo.mates(c, d)]
+    plane = [d for d in peers if topo.same_plane(c, d)]
+    far = [d for d in peers if d not in near and d not in mate and d not in plane]
+    mixed = [d for pair in zip(mate, plane) for d in pair]
+    mixed += [d for d in mate + plane if d not in mixed]
+    off = far + mixed
+    eoff = _bits(topo.mask(c, off[0]))
+    enear = [b for b in _bits(topo.mask(c, near[0])) if b not in eoff]
+    half = len(eoff) // 2
+    calls = []
+    for i in range(0, len(off), 2):
+        calls.append([(d, eoff[half * k:half * (k + 1)]) for k, d in enumerate(off[i:i + 2])])
+    calls[-1] = calls[-1] + [(near[0], enear)]
+    return off, near, eoff, enear, calls
+
+
+def rank_program(g, core, T, topo):
+    me = T.rank_of(core)
+    if me is None:
+        return
+    A = AluOpType
+    v, pe, sy = g.vector, g.tensor, g.sync
+    cnt = {}
+
+    def inc(ins, name, n=1):
+        cnt[name] = cnt.get(name, 0) + n
+        ins.then_inc(T.sem[name], n)
+
+    def wait(q, name):
+        q.wait_ge(T.sem[name], cnt[name])
+
+    def dst(d):
+        rid, pid = topo.addr(d, core)
+        return DstId(rid=rid, pnc=pid)
+
+    off, near, eoff, enear, calls = _plan(core, T.cores, topo)
+
+    inc(sy.dma_start(out=T.ent[:, :], in_=T.idx[:, :]), "ldi", 16)
+    inc(sy.dma_start(out=T.tabs[:, :], in_=T.tab[:, :]), "ldt", 16)
+
+    inc(v.memset(T.ones[:, :], 1.0), "cv")
+    inc(v.memset(T.eh[:, 0:8], 0.0), "vv")
+    inc(g.iota(T.io16[:, :], [[0, 2], [1, 8]], 0, 0, allow_small_or_imprecise_dtypes=True), "ca")
+    wait(g, "cv")
+    inc(g.affine_select(T.upper[:, :], T.ones[:, :], [[1, 128]], A.is_gt, 0.0, 0, -1), "ca")
+    inc(g.iota(T.m16[:, :], [[0, 8], [1, 16]], 0, 0, allow_small_or_imprecise_dtypes=True), "cb")
+    inc(g.iota(T.c32[:, :], [[1, QW]], 0, 0, allow_small_or_imprecise_dtypes=True), "cb")
+    inc(g.iota(T.ai[:, :], [[0, 8], [-8, 16]], 128, 1), "cc")
+    inc(g.iota(T.bi[:, :], [[1, 2], [-1, 16]], 16, 2), "cc")
+
+    wait(pe, "cv")
+    wait(pe, "ca")
+    pe.matmul(T.pc[:, 0:16], T.ones[0:64, :], T.io16[0:64, :], True, False)
+    wait(v, "ldi")
+    inc(v.tensor_scalar(out=T.oli[:, 0:2], in0=T.ent[:, :], scalar1=12, scalar2=None, op0=A.arith_shift_right), "vv")
+    inc(v.tensor_scalar(out=T.oli[:, 2:4], in0=T.ent[:, :], scalar1=R - 1, scalar2=None, op0=A.bitwise_and), "vv")
+    wait(v, "vv")
+    inc(v.tensor_copy(out=T.olf[:, :], in_=T.oli[:, :]), "vv")
+    wait(v, "vv")
+    wait(v, "ca")
+    for k in range(2):
+        inc(v.tensor_scalar(out=T.eh[:, 8 + 8 * k:16 + 8 * k], in0=T.io16[:, 0:8], scalar1=T.olf[:, k:k + 1], scalar2=None,
+                            op0=A.is_equal), "vt")
+    wait(pe, "vt")
+    pe.matmul(T.pc[:, 0:16], T.upper[:, :], T.eh[:, 8:24], False, False)
+    inc(pe.matmul(T.pc[:, 0:16], T.ones[:, :], T.eh[:, 0:16], False, True), "tv")
+    wait(v, "vt")
+    wait(v, "tv")
+    inc(v.tensor_tensor(out=T.prod[:, :], in0=T.pc[:, 0:16], in1=T.eh[:, 8:24], op=A.mult), "vv")
+    wait(v, "vv")
+    for k in range(2):
+        inc(v.tensor_reduce(out=T.slotf[:, k:k + 1], in_=T.prod[:, 8 * k:8 * k + 8], axis=AxisListType.X, op=A.add), "vv")
+    wait(v, "vv")
+    inc(v.tensor_copy(out=T.sloti[:, :], in_=T.slotf[:, :]), "vv")
+    wait(v, "vv")
+    inc(v.tensor_scalar(out=T.mdi[:, 0:2], in0=T.sloti[:, :], scalar1=15, scalar2=None, op0=A.bitwise_and), "vv")
+    inc(v.tensor_scalar(out=T.mdi[:, 2:4], in0=T.sloti[:, :], scalar1=4, scalar2=None, op0=A.arith_shift_right), "vv")
+    wait(v, "vv")
+    inc(v.tensor_copy(out=T.mdf[:, :], in_=T.mdi[:, :]), "vv")
+    wait(v, "vv")
+    wait(v, "cb")
+
+    for k in range(2):
+        inc(v.tensor_scalar(out=T.lq[:, 128 * k:128 * k + 128], in0=T.m16[:, :], scalar1=T.mdf[:, k:k + 1],
+                            scalar2=T.olf[:, 2 + k:3 + k], op0=A.is_equal, op1=A.mult), "vt")
+        inc(v.tensor_scalar(out=T.rq[:, QW * k:QW * k + QW], in0=T.c32[:, :], scalar1=T.mdf[:, 2 + k:3 + k], scalar2=None,
+                            op0=A.is_equal), "vt")
+    wait(pe, "vt")
+    pe.matmul(T.pq[:, 0:QW], T.lq[:, 0:128], T.rq[:, 0:QW], True, False)
+    inc(pe.matmul(T.pq[:, 0:QW], T.lq[:, 128:256], T.rq[:, QW:2 * QW], False, True), "tv")
+    wait(v, "tv")
+    mine = T.qall[:, QW * me:QW * me + QW]
+    inc(v.tensor_copy(out=mine, in_=T.pq[:, 0:QW]), "qs")
+
+    wait(g, "qs")
+    g.remote_dma_fused([
+        RemoteDMATransfer(dst_ids=[dst(d) for d in off], dma_engine_mask=_mask(eoff), remote_sem=T.sem.req,
+                          srcs=[mine], dsts=[mine for d in off]),
+        RemoteDMATransfer(dst_ids=[dst(near[0])], dma_engine_mask=_mask(enear), remote_sem=T.sem.req,
+                          srcs=[mine], dsts=[mine]),
+    ], local_sem=T.sem.loc)
+    left = len(eoff) + len(enear)
+    asked = 0
+    for s in T.cores:
+        if s != core:
+            soff, snear, seoff, senear, scalls = _plan(s, T.cores, topo)
+            asked += len(seoff) if core in soff else len(senear)
+
+    wait(v, "cc")
+    inc(v.tensor_scalar(out=T.ai[:, :], in0=T.ai[:, :], scalar1=3, scalar2=None, op0=A.arith_shift_right), "vv")
+    inc(v.tensor_scalar(out=T.bi[:, :], in0=T.bi[:, :], scalar1=15, scalar2=None, op0=A.bitwise_and), "vv")
+    wait(v, "vv")
+    inc(v.tensor_scalar(out=T.af[:, :], in0=T.ai[:, :], scalar1=16, scalar2=None, op0=A.is_equal), "vv")
+    inc(v.tensor_scalar(out=T.bf[:, :], in0=T.bi[:, :], scalar1=0, scalar2=None, op0=A.is_equal), "vv")
+    wait(v, "vv")
+    for k in range(2):
+        inc(v.tensor_scalar(out=T.lf[:, 128 * k:128 * k + 128], in0=T.af[:, :], scalar1=T.slotf[:, k:k + 1], scalar2=None,
+                            op0=A.mult), "vt")
+    wait(pe, "vt")
+    pe.matmul(T.pf[:, 0:16], T.lf[:, 0:128], T.bf[:, 0:16], True, False)
+    inc(pe.matmul(T.pf[:, 0:16], T.lf[:, 128:256], T.bf[:, 16:32], False, True), "tv")
+    wait(v, "tv")
+    inc(v.tensor_copy(out=T.fin[:, :], in_=T.pf[:, 0:16]), "vv")
+
+    def pick(out, q):
+        return v.tensor_copy(out=out, in_=T.tabs[:, 0:R].indirect(T.qall[:, QW * q + BW * me:QW * q + BW * me + BW]))
+
+    v.wait_ge(T.sem.req, asked)
+    wait(v, "ldt")
+    wait(v, "qs")
+    block = T.land[:, CAP * me:CAP * me + CAP]
+    for i, call in enumerate(calls):
+        for d, eng in call:
+            q = T.rank_of(d)
+            inc(pick(T.snd[:, CAP * q:CAP * q + CAP], q), "gs%d" % i)
+        wait(g, "gs%d" % i)
+        g.remote_dma_fused([
+            RemoteDMATransfer(dst_ids=[dst(d)], dma_engine_mask=_mask(eng), remote_sem=T.sem.dat,
+                              srcs=[T.snd[:, CAP * T.rank_of(d):CAP * T.rank_of(d) + CAP]], dsts=[block])
+            for d, eng in call], local_sem=T.sem.loc)
+        left += sum(len(eng) for d, eng in call)
+    inc(pick(block, me), "vv")
+
+    got = 0
+    for s in T.cores:
+        if s != core:
+            for call in _plan(s, T.cores, topo)[4]:
+                got += sum(len(eng) for d, eng in call if d == core)
+    v.wait_ge(T.sem.dat, got)
+    wait(v, "vv")
+    inc(v.tensor_copy(out=T.ysb[:, :], in_=T.land[:, 0:N * CAP].indirect(T.fin[:, 0:16])), "done")
+    wait(sy, "done")
+    inc(sy.dma_start(out=T.y[:, :], in_=T.ysb[:, :]), "st", 16)
+    g.wait_ge(T.sem.loc, left)
+    wait(g, "st")

@@ -1,29 +1,36 @@
 from concourse.bass import DstId, RemoteDMATransfer
-from concourse.mybir import AluOpType, AxisListType
+from concourse.mybir import AluOpType, AxisListType, ActivationFunctionType
 
 N, R, L, CAP = 8, 4096, 256, 64
 BW = CAP // 16
 QW = N * BW
+LO = 64
+BIG = N * CAP
 
 SCRATCH = {
     "tabs": ("sbuf", [128, R], "float32"),
     "ent": ("sbuf", [128, 2], "int32"),
-    "oli": ("sbuf", [128, 4], "int32"),
-    "olf": ("sbuf", [128, 4], "float32"),
-    "eh": ("sbuf", [128, 24], "float32"),
-    "ones": ("sbuf", [128, 128], "float32"),
-    "upper": ("sbuf", [128, 128], "float32"),
-    "io16": ("sbuf", [128, 16], "float32"),
-    "m16": ("sbuf", [128, 128], "float32"),
-    "c32": ("sbuf", [128, QW], "float32"),
-    "prod": ("sbuf", [128, 16], "float32"),
+    "oli": ("sbuf", [128, 6], "int32"),
+    "olf": ("sbuf", [128, 6], "float32"),
+    "eh": ("sbuf", [128, 24], "bfloat16"),
+    "onesb": ("sbuf", [128, 128], "bfloat16"),
+    "dd": ("sbuf", [128, 128], "bfloat16"),
+    "upperb": ("sbuf", [128, 128], "bfloat16"),
+    "diagb": ("sbuf", [128, 128], "bfloat16"),
+    "upd": ("sbuf", [128, 128], "bfloat16"),
+    "io16b": ("sbuf", [128, 16], "bfloat16"),
+    "m16b": ("sbuf", [128, 128], "bfloat16"),
+    "m8b": ("sbuf", [128, 128], "bfloat16"),
+    "cs2": ("sbuf", [128, QW], "float32"),
+    "c2b": ("sbuf", [128, QW], "bfloat16"),
     "slotf": ("sbuf", [128, 2], "float32"),
-    "sloti": ("sbuf", [128, 2], "int32"),
-    "mdi": ("sbuf", [128, 4], "int32"),
-    "mdf": ("sbuf", [128, 4], "float32"),
-    "lq": ("sbuf", [128, 256], "float32"),
-    "rq": ("sbuf", [128, 2 * QW], "float32"),
-    "qall": ("sbuf", [128, N * QW], "uint16"),
+    "sl8": ("sbuf", [128, 2], "float32"),
+    "junk": ("sbuf", [128, 2 * QW], "float32"),
+    "a2": ("sbuf", [128, 2], "float32"),
+    "lq": ("sbuf", [128, 256], "bfloat16"),
+    "rq": ("sbuf", [128, 4 * QW], "bfloat16"),
+    "qm": ("sbuf", [128, QW], "uint16"),
+    "qin": ("sbuf", [128, 8 * N], "uint16"),
     "ai": ("sbuf", [128, 128], "int32"),
     "af": ("sbuf", [128, 128], "float32"),
     "bi": ("sbuf", [128, 32], "int32"),
@@ -37,8 +44,8 @@ SCRATCH = {
     "pq": ("psum", [128, 512], "float32"),
     "pf": ("psum", [128, 512], "float32"),
 }
-SEMAPHORES = ["ldi", "ldt", "cv", "ca", "cb", "cc", "vv", "vt", "tv", "qs", "gs0", "gs1", "gs2", "gs3", "done", "st",
-              "req", "dat", "loc"]
+SEMAPHORES = ["ldi", "ldt", "cv", "ca", "cb", "cc", "cd", "cu", "vv", "vt", "tv", "sl", "sa0", "sa1", "vq0", "vq1", "qs", "fs",
+              "own", "gs0", "gs1", "gs2", "done", "st", "req0", "req1", "req2", "req3", "dat", "loc"]
 
 
 def _bits(m):
@@ -55,17 +62,19 @@ def _plan(c, cores, topo):
     mate = [d for d in peers if topo.mates(c, d)]
     plane = [d for d in peers if topo.same_plane(c, d)]
     far = [d for d in peers if d not in near and d not in mate and d not in plane]
-    mixed = [d for pair in zip(mate, plane) for d in pair]
-    mixed += [d for d in mate + plane if d not in mixed]
-    off = far + mixed
-    eoff = _bits(topo.mask(c, off[0]))
+
+    def mine(l):
+        return [d for d in l if topo.die(d) == topo.die(c)]
+
+    def other(l):
+        return [d for d in l if topo.die(d) != topo.die(c)]
+
+    groups = [mine(far) + other(far), mine(mate) + mine(plane), other(mate) + other(plane)]
+    eoff = _bits(topo.mask(c, far[0]))
     enear = [b for b in _bits(topo.mask(c, near[0])) if b not in eoff]
     half = len(eoff) // 2
-    calls = []
-    for i in range(0, len(off), 2):
-        calls.append([(d, eoff[half * k:half * (k + 1)]) for k, d in enumerate(off[i:i + 2])])
-    calls[-1] = calls[-1] + [(near[0], enear)]
-    return off, near, eoff, enear, calls
+    stages = [[(d, eoff[half * k:half * (k + 1)]) for k, d in enumerate(grp)] for grp in groups]
+    return stages, (near[0], enear)
 
 
 def rank_program(g, core, T, topo):
@@ -73,7 +82,8 @@ def rank_program(g, core, T, topo):
     if me is None:
         return
     A = AluOpType
-    v, pe, sy = g.vector, g.tensor, g.sync
+    AF = ActivationFunctionType
+    v, pe, sy, sc = g.vector, g.tensor, g.sync, g.scalar
     cnt = {}
 
     def inc(ins, name, n=1):
@@ -87,78 +97,95 @@ def rank_program(g, core, T, topo):
         rid, pid = topo.addr(d, core)
         return DstId(rid=rid, pnc=pid)
 
-    off, near, eoff, enear, calls = _plan(core, T.cores, topo)
+    stages, (nearc, enear) = _plan(core, T.cores, topo)
+    NS = len(stages)
+    arrive = [0] * (NS + 1)
+    for s in T.cores:
+        if s != core:
+            sst, (sn, sen) = _plan(s, T.cores, topo)
+            for i, stage in enumerate(sst):
+                arrive[i] += sum(len(eng) for d, eng in stage if d == core)
+            if sn == core:
+                arrive[NS] += len(sen)
 
     inc(sy.dma_start(out=T.ent[:, :], in_=T.idx[:, :]), "ldi", 16)
     inc(sy.dma_start(out=T.tabs[:, :], in_=T.tab[:, :]), "ldt", 16)
 
-    inc(v.memset(T.ones[:, :], 1.0), "cv")
-    inc(v.memset(T.eh[:, 0:8], 0.0), "vv")
-    inc(g.iota(T.io16[:, :], [[0, 2], [1, 8]], 0, 0, allow_small_or_imprecise_dtypes=True), "ca")
-    wait(g, "cv")
-    inc(g.affine_select(T.upper[:, :], T.ones[:, :], [[1, 128]], A.is_gt, 0.0, 0, -1), "ca")
-    inc(g.iota(T.m16[:, :], [[0, 8], [1, 16]], 0, 0, allow_small_or_imprecise_dtypes=True), "cb")
-    inc(g.iota(T.c32[:, :], [[1, QW]], 0, 0, allow_small_or_imprecise_dtypes=True), "cb")
+    inc(v.memset(T.onesb[:, :], 1.0), "cv")
+    inc(v.memset(T.eh[:, 0:8], 0.0), "cv")
+    inc(g.iota(T.io16b[:, :], [[0, 2], [1, 8]], 0, 0, allow_small_or_imprecise_dtypes=True), "ca")
+    inc(g.iota(T.dd[:, :], [[1, 128]], 0, -1, allow_small_or_imprecise_dtypes=True), "cd")
+    inc(g.iota(T.m16b[:, :], [[0, 8], [1, 16]], 0, 0, allow_small_or_imprecise_dtypes=True), "cd")
+    inc(g.iota(T.cs2[:, :], [[32, QW]], 32 + 2 * BIG - 1, 0, allow_small_or_imprecise_dtypes=True), "cb")
+    inc(g.iota(T.c2b[:, :], [[2, QW]], -QW, 0, allow_small_or_imprecise_dtypes=True), "cb")
     inc(g.iota(T.ai[:, :], [[0, 8], [-8, 16]], 128, 1), "cc")
     inc(g.iota(T.bi[:, :], [[1, 2], [-1, 16]], 16, 2), "cc")
+    wait(v, "cd")
+    inc(v.tensor_scalar(out=T.upperb[:, :], in0=T.dd[:, :], scalar1=0.0, scalar2=None, op0=A.is_gt), "cu")
+    inc(v.tensor_scalar(out=T.diagb[:, :], in0=T.dd[:, :], scalar1=0.0, scalar2=float(BIG), op0=A.is_equal, op1=A.mult), "cu")
+    inc(v.tensor_scalar(out=T.m8b[:, :], in0=T.m16b[:, :], scalar1=0.125, scalar2=None, op0=A.mult), "cu")
+    wait(v, "cu")
+    inc(v.tensor_tensor(out=T.upd[:, :], in0=T.upperb[:, :], in1=T.diagb[:, :], op=A.add), "ca")
 
     wait(pe, "cv")
     wait(pe, "ca")
-    pe.matmul(T.pc[:, 0:16], T.ones[0:64, :], T.io16[0:64, :], True, False)
+    pe.matmul(T.pc[:, 0:16], T.onesb[0:64, :], T.io16b[0:64, :], True, False)
     wait(v, "ldi")
     inc(v.tensor_scalar(out=T.oli[:, 0:2], in0=T.ent[:, :], scalar1=12, scalar2=None, op0=A.arith_shift_right), "vv")
-    inc(v.tensor_scalar(out=T.oli[:, 2:4], in0=T.ent[:, :], scalar1=R - 1, scalar2=None, op0=A.bitwise_and), "vv")
     wait(v, "vv")
-    inc(v.tensor_copy(out=T.olf[:, :], in_=T.oli[:, :]), "vv")
+    inc(v.tensor_copy(out=T.olf[:, 0:2], in_=T.oli[:, 0:2]), "vv")
     wait(v, "vv")
     wait(v, "ca")
     for k in range(2):
-        inc(v.tensor_scalar(out=T.eh[:, 8 + 8 * k:16 + 8 * k], in0=T.io16[:, 0:8], scalar1=T.olf[:, k:k + 1], scalar2=None,
+        inc(v.tensor_scalar(out=T.eh[:, 8 + 8 * k:16 + 8 * k], in0=T.io16b[:, 0:8], scalar1=T.olf[:, k:k + 1], scalar2=None,
                             op0=A.is_equal), "vt")
     wait(pe, "vt")
-    pe.matmul(T.pc[:, 0:16], T.upper[:, :], T.eh[:, 8:24], False, False)
-    inc(pe.matmul(T.pc[:, 0:16], T.ones[:, :], T.eh[:, 0:16], False, True), "tv")
-    wait(v, "vt")
+    pe.matmul(T.pc[:, 0:16], T.upd[:, :], T.eh[:, 8:24], False, False)
+    inc(pe.matmul(T.pc[:, 0:16], T.onesb[:, :], T.eh[:, 0:16], False, True), "tv")
+    inc(v.tensor_scalar(out=T.oli[:, 2:4], in0=T.ent[:, :], scalar1=(R - 1) - (LO - 1), scalar2=None, op0=A.bitwise_and), "vv")
+    inc(v.tensor_scalar(out=T.oli[:, 4:6], in0=T.ent[:, :], scalar1=LO - 1, scalar2=None, op0=A.bitwise_and), "vv")
+    wait(v, "vv")
+    inc(v.tensor_copy(out=T.olf[:, 2:6], in_=T.oli[:, 2:6]), "vv")
     wait(v, "tv")
-    inc(v.tensor_tensor(out=T.prod[:, :], in0=T.pc[:, 0:16], in1=T.eh[:, 8:24], op=A.mult), "vv")
-    wait(v, "vv")
     for k in range(2):
-        inc(v.tensor_reduce(out=T.slotf[:, k:k + 1], in_=T.prod[:, 8 * k:8 * k + 8], axis=AxisListType.X, op=A.add), "vv")
-    wait(v, "vv")
-    inc(v.tensor_copy(out=T.sloti[:, :], in_=T.slotf[:, :]), "vv")
-    wait(v, "vv")
-    inc(v.tensor_scalar(out=T.mdi[:, 0:2], in0=T.sloti[:, :], scalar1=15, scalar2=None, op0=A.bitwise_and), "vv")
-    inc(v.tensor_scalar(out=T.mdi[:, 2:4], in0=T.sloti[:, :], scalar1=4, scalar2=None, op0=A.arith_shift_right), "vv")
-    wait(v, "vv")
-    inc(v.tensor_copy(out=T.mdf[:, :], in_=T.mdi[:, :]), "vv")
+        inc(v.tensor_reduce(out=T.slotf[:, k:k + 1], in_=T.pc[:, 8 * k:8 * k + 8], axis=AxisListType.X, op=A.max), "sl")
+    wait(sc, "sl")
+    wait(sc, "cb")
+    for k in range(2):
+        inc(sc.activation(out=T.junk[:, QW * k:QW * k + QW], in_=T.cs2[:, :], func=AF.Sign, bias=T.slotf[:, k:k + 1], scale=-0.5,
+                          accum_out=T.a2[:, k:k + 1]), "sa%d" % k)
+    wait(v, "sl")
+    inc(v.tensor_scalar(out=T.sl8[:, :], in0=T.slotf[:, :], scalar1=0.125, scalar2=-float(BIG // 8 + QW), op0=A.mult, op1=A.add),
+        "vv")
     wait(v, "vv")
     wait(v, "cb")
 
+    last = None
     for k in range(2):
-        inc(v.tensor_scalar(out=T.lq[:, 128 * k:128 * k + 128], in0=T.m16[:, :], scalar1=T.mdf[:, k:k + 1],
-                            scalar2=T.olf[:, 2 + k:3 + k], op0=A.is_equal, op1=A.mult), "vt")
-        inc(v.tensor_scalar(out=T.rq[:, QW * k:QW * k + QW], in0=T.c32[:, :], scalar1=T.mdf[:, 2 + k:3 + k], scalar2=None,
-                            op0=A.is_equal), "vt")
-    wait(pe, "vt")
-    pe.matmul(T.pq[:, 0:QW], T.lq[:, 0:128], T.rq[:, 0:QW], True, False)
-    inc(pe.matmul(T.pq[:, 0:QW], T.lq[:, 128:256], T.rq[:, QW:2 * QW], False, True), "tv")
+        lq = T.lq[:, 128 * k:128 * k + 128]
+        wait(v, "sa%d" % k)
+        inc(v.tensor_scalar(out=lq, in0=T.m8b[:, :], scalar1=T.a2[:, k:k + 1], scalar2=T.sl8[:, k:k + 1],
+                            op0=A.add, op1=A.is_equal), "vq%d" % k)
+        for h in range(2):
+            inc(v.tensor_scalar(out=T.rq[:, QW * (2 * k + h):QW * (2 * k + h + 1)], in0=T.c2b[:, :], scalar1=T.a2[:, k:k + 1],
+                                scalar2=T.olf[:, 2 + 2 * h + k:3 + 2 * h + k], op0=A.is_equal, op1=A.mult), "vq%d" % k)
+        wait(pe, "vq%d" % k)
+        for h in range(2):
+            last = pe.matmul(T.pq[:, 0:QW], lq, T.rq[:, QW * (2 * k + h):QW * (2 * k + h + 1)], k == 0 and h == 0,
+                             k == 1 and h == 1)
+    inc(last, "tv")
     wait(v, "tv")
-    mine = T.qall[:, QW * me:QW * me + QW]
-    inc(v.tensor_copy(out=mine, in_=T.pq[:, 0:QW]), "qs")
+    inc(v.tensor_copy(out=T.qm[:, :], in_=T.pq[:, 0:QW]), "qs")
 
+    here = T.qin[:, 8 * me:8 * me + BW]
+    left = 0
     wait(g, "qs")
-    g.remote_dma_fused([
-        RemoteDMATransfer(dst_ids=[dst(d) for d in off], dma_engine_mask=_mask(eoff), remote_sem=T.sem.req,
-                          srcs=[mine], dsts=[mine for d in off]),
-        RemoteDMATransfer(dst_ids=[dst(near[0])], dma_engine_mask=_mask(enear), remote_sem=T.sem.req,
-                          srcs=[mine], dsts=[mine]),
-    ], local_sem=T.sem.loc)
-    left = len(eoff) + len(enear)
-    asked = 0
-    for s in T.cores:
-        if s != core:
-            soff, snear, seoff, senear, scalls = _plan(s, T.cores, topo)
-            asked += len(seoff) if core in soff else len(senear)
+    for i, stage in enumerate(stages + [[(nearc, enear)]]):
+        g.remote_dma_fused([
+            RemoteDMATransfer(dst_ids=[dst(d)], dma_engine_mask=_mask(eng), remote_sem=T.sem["req%d" % i],
+                              srcs=[T.qm[:, BW * T.rank_of(d):BW * T.rank_of(d) + BW]], dsts=[here])
+            for d, eng in stage], local_sem=T.sem.loc)
+        left += sum(len(eng) for d, eng in stage)
 
     wait(v, "cc")
     inc(v.tensor_scalar(out=T.ai[:, :], in0=T.ai[:, :], scalar1=3, scalar2=None, op0=A.arith_shift_right), "vv")
@@ -174,35 +201,48 @@ def rank_program(g, core, T, topo):
     pe.matmul(T.pf[:, 0:16], T.lf[:, 0:128], T.bf[:, 0:16], True, False)
     inc(pe.matmul(T.pf[:, 0:16], T.lf[:, 128:256], T.bf[:, 16:32], False, True), "tv")
     wait(v, "tv")
-    inc(v.tensor_copy(out=T.fin[:, :], in_=T.pf[:, 0:16]), "vv")
+    inc(v.tensor_scalar(out=T.fin[:, :], in0=T.pf[:, 0:16], scalar1=-float(BIG), scalar2=None, op0=A.add), "fs")
 
-    def pick(out, q):
-        return v.tensor_copy(out=out, in_=T.tabs[:, 0:R].indirect(T.qall[:, QW * q + BW * me:QW * q + BW * me + BW]))
+    def vpick(out, win, offs):
+        return v.tensor_copy(out=out, in_=win.indirect(offs))
 
-    v.wait_ge(T.sem.req, asked)
+    def spick(out, win, offs):
+        return sc.activation(out=out, in_=win.indirect(offs), func=AF.Copy)
+
+    def asked(d, a=0, b=BW):
+        q = T.rank_of(d)
+        return T.snd[:, CAP * q + 16 * a:CAP * q + 16 * b], T.tabs[:, 0:R], T.qin[:, 8 * q + a:8 * q + b]
+
     wait(v, "ldt")
-    wait(v, "qs")
+    wait(sc, "ldt")
     block = T.land[:, CAP * me:CAP * me + CAP]
-    for i, call in enumerate(calls):
-        for d, eng in call:
-            q = T.rank_of(d)
-            inc(pick(T.snd[:, CAP * q:CAP * q + CAP], q), "gs%d" % i)
+    for i, stage in enumerate(stages):
+        v.wait_ge(T.sem["req%d" % i], arrive[i])
+        sc.wait_ge(T.sem["req%d" % i], arrive[i])
+        inc(vpick(*asked(stage[0][0])), "gs%d" % i)
+        inc(spick(*asked(stage[1][0])), "gs%d" % i)
+        call = list(stage)
+        if i == NS - 1:
+            v.wait_ge(T.sem["req%d" % NS], arrive[NS])
+            sc.wait_ge(T.sem["req%d" % NS], arrive[NS])
+            inc(vpick(*asked(nearc, 0, BW // 2)), "gs%d" % i)
+            inc(spick(*asked(nearc, BW // 2, BW)), "gs%d" % i)
+            call.append((nearc, enear))
         wait(g, "gs%d" % i)
         g.remote_dma_fused([
             RemoteDMATransfer(dst_ids=[dst(d)], dma_engine_mask=_mask(eng), remote_sem=T.sem.dat,
                               srcs=[T.snd[:, CAP * T.rank_of(d):CAP * T.rank_of(d) + CAP]], dsts=[block])
             for d, eng in call], local_sem=T.sem.loc)
         left += sum(len(eng) for d, eng in call)
-    inc(pick(block, me), "vv")
+    wait(v, "qs")
+    inc(vpick(block, T.tabs[:, 0:R], T.qm[:, BW * me:BW * me + BW]), "own")
 
-    got = 0
-    for s in T.cores:
-        if s != core:
-            for call in _plan(s, T.cores, topo)[4]:
-                got += sum(len(eng) for d, eng in call if d == core)
-    v.wait_ge(T.sem.dat, got)
-    wait(v, "vv")
-    inc(v.tensor_copy(out=T.ysb[:, :], in_=T.land[:, 0:N * CAP].indirect(T.fin[:, 0:16])), "done")
+    got = sum(arrive)
+    for q, pick, h in ((v, vpick, 0), (sc, spick, 1)):
+        q.wait_ge(T.sem.dat, got)
+        wait(q, "own")
+        wait(q, "fs")
+        inc(pick(T.ysb[:, 128 * h:128 * h + 128], T.land[:, 0:N * CAP], T.fin[:, 8 * h:8 * h + 8]), "done")
     wait(sy, "done")
     inc(sy.dma_start(out=T.y[:, :], in_=T.ysb[:, :]), "st", 16)
     g.wait_ge(T.sem.loc, left)

@@ -4,14 +4,14 @@ from concourse.mybir import AluOpType, AxisListType, ActivationFunctionType
 N, R, L, CAP = 8, 4096, 256, 64
 BW = CAP // 16
 QW = N * BW
-LO = 64
+MID = R // 2
 BIG = N * CAP
 
 SCRATCH = {
     "tabs": ("sbuf", [128, R], "float32"),
     "ent": ("sbuf", [128, 2], "int32"),
-    "oli": ("sbuf", [128, 6], "int32"),
-    "olf": ("sbuf", [128, 6], "float32"),
+    "oli": ("sbuf", [128, 4], "int32"),
+    "olf": ("sbuf", [128, 4], "float32"),
     "eh": ("sbuf", [128, 24], "bfloat16"),
     "onesb": ("sbuf", [128, 128], "bfloat16"),
     "dd": ("sbuf", [128, 128], "bfloat16"),
@@ -27,8 +27,8 @@ SCRATCH = {
     "sl8": ("sbuf", [128, 2], "float32"),
     "junk": ("sbuf", [128, 2 * QW], "float32"),
     "a2": ("sbuf", [128, 2], "float32"),
-    "lq": ("sbuf", [128, 256], "bfloat16"),
-    "rq": ("sbuf", [128, 4 * QW], "bfloat16"),
+    "lq": ("sbuf", [128, 256], "float16"),
+    "rq": ("sbuf", [128, 2 * QW], "float16"),
     "qm": ("sbuf", [128, QW], "uint16"),
     "qin": ("sbuf", [128, 8 * N], "uint16"),
     "ai": ("sbuf", [128, 128], "int32"),
@@ -44,8 +44,8 @@ SCRATCH = {
     "pq": ("psum", [128, 512], "float32"),
     "pf": ("psum", [128, 512], "float32"),
 }
-SEMAPHORES = ["ldi", "ldt", "cv", "ca", "cb", "cc", "cd", "cu", "vv", "vt", "tv", "sl", "sa0", "sa1", "vq0", "vq1", "qs", "fs",
-              "own", "gs0", "gs1", "gs2", "done", "st", "req0", "req1", "req2", "req3", "dat", "loc"]
+SEMAPHORES = ["ldi", "ldt", "cv", "ca", "cb", "cc", "cd", "ci", "cm", "c8", "cu", "vv", "vt", "tv", "sl", "sa0", "sa1", "vq0",
+              "vq1", "qs", "fs", "own", "gs0", "gs1", "gs2", "done", "st", "req0", "req1", "req2", "req3", "dat", "loc"]
 
 
 def _bits(m):
@@ -113,9 +113,9 @@ def rank_program(g, core, T, topo):
 
     inc(v.memset(T.onesb[:, :], 1.0), "cv")
     inc(v.memset(T.eh[:, 0:8], 0.0), "cv")
-    inc(g.iota(T.io16b[:, :], [[0, 2], [1, 8]], 0, 0, allow_small_or_imprecise_dtypes=True), "ca")
     inc(g.iota(T.dd[:, :], [[1, 128]], 0, -1, allow_small_or_imprecise_dtypes=True), "cd")
-    inc(g.iota(T.m16b[:, :], [[0, 8], [1, 16]], 0, 0, allow_small_or_imprecise_dtypes=True), "cd")
+    inc(g.iota(T.io16b[:, :], [[0, 2], [1, 8]], 0, 0, allow_small_or_imprecise_dtypes=True), "ci")
+    inc(g.iota(T.m16b[:, :], [[0, 8], [1, 16]], 0, 0, allow_small_or_imprecise_dtypes=True), "cm")
     inc(g.iota(T.cs2[:, :], [[32, QW]], 32 + 2 * BIG - 1, 0, allow_small_or_imprecise_dtypes=True), "cb")
     inc(g.iota(T.c2b[:, :], [[2, QW]], -QW, 0, allow_small_or_imprecise_dtypes=True), "cb")
     inc(g.iota(T.ai[:, :], [[0, 8], [-8, 16]], 128, 1), "cc")
@@ -123,29 +123,30 @@ def rank_program(g, core, T, topo):
     wait(v, "cd")
     inc(v.tensor_scalar(out=T.upperb[:, :], in0=T.dd[:, :], scalar1=0.0, scalar2=None, op0=A.is_gt), "cu")
     inc(v.tensor_scalar(out=T.diagb[:, :], in0=T.dd[:, :], scalar1=0.0, scalar2=float(BIG), op0=A.is_equal, op1=A.mult), "cu")
-    inc(v.tensor_scalar(out=T.m8b[:, :], in0=T.m16b[:, :], scalar1=0.125, scalar2=None, op0=A.mult), "cu")
     wait(v, "cu")
     inc(v.tensor_tensor(out=T.upd[:, :], in0=T.upperb[:, :], in1=T.diagb[:, :], op=A.add), "ca")
+    wait(sc, "cm")
+    inc(sc.activation(out=T.m8b[:, :], in_=T.m16b[:, :], func=AF.Copy, scale=0.125), "c8")
 
     wait(pe, "cv")
-    wait(pe, "ca")
+    wait(pe, "ci")
     pe.matmul(T.pc[:, 0:16], T.onesb[0:64, :], T.io16b[0:64, :], True, False)
     wait(v, "ldi")
     inc(v.tensor_scalar(out=T.oli[:, 0:2], in0=T.ent[:, :], scalar1=12, scalar2=None, op0=A.arith_shift_right), "vv")
     wait(v, "vv")
     inc(v.tensor_copy(out=T.olf[:, 0:2], in_=T.oli[:, 0:2]), "vv")
     wait(v, "vv")
-    wait(v, "ca")
+    wait(v, "ci")
     for k in range(2):
         inc(v.tensor_scalar(out=T.eh[:, 8 + 8 * k:16 + 8 * k], in0=T.io16b[:, 0:8], scalar1=T.olf[:, k:k + 1], scalar2=None,
                             op0=A.is_equal), "vt")
+    wait(pe, "ca")
     wait(pe, "vt")
     pe.matmul(T.pc[:, 0:16], T.upd[:, :], T.eh[:, 8:24], False, False)
     inc(pe.matmul(T.pc[:, 0:16], T.onesb[:, :], T.eh[:, 0:16], False, True), "tv")
-    inc(v.tensor_scalar(out=T.oli[:, 2:4], in0=T.ent[:, :], scalar1=(R - 1) - (LO - 1), scalar2=None, op0=A.bitwise_and), "vv")
-    inc(v.tensor_scalar(out=T.oli[:, 4:6], in0=T.ent[:, :], scalar1=LO - 1, scalar2=None, op0=A.bitwise_and), "vv")
+    inc(v.tensor_scalar(out=T.oli[:, 2:4], in0=T.ent[:, :], scalar1=R - 1, scalar2=None, op0=A.bitwise_and), "vv")
     wait(v, "vv")
-    inc(v.tensor_copy(out=T.olf[:, 2:6], in_=T.oli[:, 2:6]), "vv")
+    inc(v.tensor_scalar(out=T.olf[:, 2:4], in0=T.oli[:, 2:4], scalar1=-float(MID), scalar2=None, op0=A.add), "vv")
     wait(v, "tv")
     for k in range(2):
         inc(v.tensor_reduce(out=T.slotf[:, k:k + 1], in_=T.pc[:, 8 * k:8 * k + 8], axis=AxisListType.X, op=A.max), "sl")
@@ -159,23 +160,22 @@ def rank_program(g, core, T, topo):
         "vv")
     wait(v, "vv")
     wait(v, "cb")
+    wait(v, "c8")
 
     last = None
     for k in range(2):
         lq = T.lq[:, 128 * k:128 * k + 128]
+        rq = T.rq[:, QW * k:QW * k + QW]
         wait(v, "sa%d" % k)
         inc(v.tensor_scalar(out=lq, in0=T.m8b[:, :], scalar1=T.a2[:, k:k + 1], scalar2=T.sl8[:, k:k + 1],
                             op0=A.add, op1=A.is_equal), "vq%d" % k)
-        for h in range(2):
-            inc(v.tensor_scalar(out=T.rq[:, QW * (2 * k + h):QW * (2 * k + h + 1)], in0=T.c2b[:, :], scalar1=T.a2[:, k:k + 1],
-                                scalar2=T.olf[:, 2 + 2 * h + k:3 + 2 * h + k], op0=A.is_equal, op1=A.mult), "vq%d" % k)
+        inc(v.tensor_scalar(out=rq, in0=T.c2b[:, :], scalar1=T.a2[:, k:k + 1], scalar2=T.olf[:, 2 + k:3 + k],
+                            op0=A.is_equal, op1=A.mult), "vq%d" % k)
         wait(pe, "vq%d" % k)
-        for h in range(2):
-            last = pe.matmul(T.pq[:, 0:QW], lq, T.rq[:, QW * (2 * k + h):QW * (2 * k + h + 1)], k == 0 and h == 0,
-                             k == 1 and h == 1)
+        last = pe.matmul(T.pq[:, 0:QW], lq, rq, k == 0, k == 1)
     inc(last, "tv")
     wait(v, "tv")
-    inc(v.tensor_copy(out=T.qm[:, :], in_=T.pq[:, 0:QW]), "qs")
+    inc(v.tensor_scalar(out=T.qm[:, :], in0=T.pq[:, 0:QW], scalar1=float(MID), scalar2=None, op0=A.add), "qs")
 
     here = T.qin[:, 8 * me:8 * me + BW]
     left = 0

from concourse.bass import DstId, RemoteDMATransfer
from concourse.mybir import AluOpType, AxisListType, ActivationFunctionType

N, R, L, CAP = 8, 4096, 256, 64
BW = CAP // 16
QW = N * BW
MID = R // 2
BIG = N * CAP

SCRATCH = {
    "tabs": ("sbuf", [128, R], "float32"),
    "ent": ("sbuf", [128, 2], "int32"),
    "oli": ("sbuf", [128, 4], "int32"),
    "olf": ("sbuf", [128, 4], "float32"),
    "eh": ("sbuf", [128, 24], "bfloat16"),
    "onesb": ("sbuf", [128, 128], "bfloat16"),
    "dd": ("sbuf", [128, 128], "bfloat16"),
    "upperb": ("sbuf", [128, 128], "bfloat16"),
    "diagb": ("sbuf", [128, 128], "bfloat16"),
    "upd": ("sbuf", [128, 128], "bfloat16"),
    "io16b": ("sbuf", [128, 16], "bfloat16"),
    "m16b": ("sbuf", [128, 128], "bfloat16"),
    "m8b": ("sbuf", [128, 128], "bfloat16"),
    "cs2": ("sbuf", [128, QW], "float32"),
    "c2b": ("sbuf", [128, QW], "bfloat16"),
    "slotf": ("sbuf", [128, 2], "float32"),
    "sl8": ("sbuf", [128, 2], "float32"),
    "junk": ("sbuf", [128, 2 * QW], "float32"),
    "a2": ("sbuf", [128, 2], "float32"),
    "lq": ("sbuf", [128, 256], "float16"),
    "rq": ("sbuf", [128, 2 * QW], "float16"),
    "qm": ("sbuf", [128, QW], "uint16"),
    "qin": ("sbuf", [128, 8 * N], "uint16"),
    "ai": ("sbuf", [128, 128], "int32"),
    "af": ("sbuf", [128, 128], "float32"),
    "bi": ("sbuf", [128, 32], "int32"),
    "bf": ("sbuf", [128, 32], "float32"),
    "lf": ("sbuf", [128, 256], "float32"),
    "fin": ("sbuf", [128, 16], "uint16"),
    "snd": ("sbuf", [128, N * CAP], "float32"),
    "land": ("sbuf", [128, N * CAP], "float32"),
    "ysb": ("sbuf", [128, L], "float32"),
    "pc": ("psum", [128, 512], "float32"),
    "pq": ("psum", [128, 512], "float32"),
    "pf": ("psum", [128, 512], "float32"),
}
SEMAPHORES = ["ldi", "ldt", "cv", "ca", "cb", "cc", "cd", "ci", "cm", "c8", "cu", "vv", "vt", "tv", "sl", "sa0", "sa1", "vq0",
              "vq1", "qs", "fs", "own", "gs0", "gs1", "gs2", "done", "st", "req0", "req1", "req2", "req3", "dat", "loc"]


def _bits(m):
    return [b for b in range(m.bit_length()) if (m >> b) & 1]


def _mask(engines):
    return sum(1 << b for b in engines)


def _plan(c, cores, topo):
    peers = [d for d in cores if d != c]
    near = [d for d in peers if topo.host(d) == topo.host(c) and topo.chip(d) == topo.chip(c)]
    mate = [d for d in peers if topo.mates(c, d)]
    plane = [d for d in peers if topo.same_plane(c, d)]
    far = [d for d in peers if d not in near and d not in mate and d not in plane]

    def mine(l):
        return [d for d in l if topo.die(d) == topo.die(c)]

    def other(l):
        return [d for d in l if topo.die(d) != topo.die(c)]

    groups = [mine(far) + other(far), mine(mate) + mine(plane), other(mate) + other(plane)]
    eoff = _bits(topo.mask(c, far[0]))
    enear = [b for b in _bits(topo.mask(c, near[0])) if b not in eoff]
    half = len(eoff) // 2
    stages = [[(d, eoff[half * k:half * (k + 1)]) for k, d in enumerate(grp)] for grp in groups]
    return stages, (near[0], enear)


def rank_program(g, core, T, topo):
    me = T.rank_of(core)
    if me is None:
        return
    A = AluOpType
    AF = ActivationFunctionType
    v, pe, sy, sc = g.vector, g.tensor, g.sync, g.scalar
    cnt = {}

    def inc(ins, name, n=1):
        cnt[name] = cnt.get(name, 0) + n
        ins.then_inc(T.sem[name], n)

    def wait(q, name):
        q.wait_ge(T.sem[name], cnt[name])

    def dst(d):
        rid, pid = topo.addr(d, core)
        return DstId(rid=rid, pnc=pid)

    stages, (nearc, enear) = _plan(core, T.cores, topo)
    NS = len(stages)
    arrive = [0] * (NS + 1)
    for s in T.cores:
        if s != core:
            sst, (sn, sen) = _plan(s, T.cores, topo)
            for i, stage in enumerate(sst):
                arrive[i] += sum(len(eng) for d, eng in stage if d == core)
            if sn == core:
                arrive[NS] += len(sen)

    inc(sy.dma_start(out=T.ent[:, :], in_=T.idx[:, :]), "ldi", 16)
    inc(sy.dma_start(out=T.tabs[:, :], in_=T.tab[:, :]), "ldt", 16)

    inc(v.memset(T.onesb[:, :], 1.0), "cv")
    inc(v.memset(T.eh[:, 0:8], 0.0), "cv")
    inc(g.iota(T.dd[:, :], [[1, 128]], 0, -1, allow_small_or_imprecise_dtypes=True), "cd")
    inc(g.iota(T.io16b[:, :], [[0, 2], [1, 8]], 0, 0, allow_small_or_imprecise_dtypes=True), "ci")
    inc(g.iota(T.m16b[:, :], [[0, 8], [1, 16]], 0, 0, allow_small_or_imprecise_dtypes=True), "cm")
    inc(g.iota(T.cs2[:, :], [[32, QW]], 32 + 2 * BIG - 1, 0, allow_small_or_imprecise_dtypes=True), "cb")
    inc(g.iota(T.c2b[:, :], [[2, QW]], -QW, 0, allow_small_or_imprecise_dtypes=True), "cb")
    inc(g.iota(T.ai[:, :], [[0, 8], [-8, 16]], 128, 1), "cc")
    inc(g.iota(T.bi[:, :], [[1, 2], [-1, 16]], 16, 2), "cc")
    wait(v, "cd")
    inc(v.tensor_scalar(out=T.upperb[:, :], in0=T.dd[:, :], scalar1=0.0, scalar2=None, op0=A.is_gt), "cu")
    inc(v.tensor_scalar(out=T.diagb[:, :], in0=T.dd[:, :], scalar1=0.0, scalar2=float(BIG), op0=A.is_equal, op1=A.mult), "cu")
    wait(v, "cu")
    inc(v.tensor_tensor(out=T.upd[:, :], in0=T.upperb[:, :], in1=T.diagb[:, :], op=A.add), "ca")
    wait(sc, "cm")
    inc(sc.activation(out=T.m8b[:, :], in_=T.m16b[:, :], func=AF.Copy, scale=0.125), "c8")

    wait(pe, "cv")
    wait(pe, "ci")
    pe.matmul(T.pc[:, 0:16], T.onesb[0:64, :], T.io16b[0:64, :], True, False)
    wait(v, "ldi")
    inc(v.tensor_scalar(out=T.oli[:, 0:2], in0=T.ent[:, :], scalar1=12, scalar2=None, op0=A.arith_shift_right), "vv")
    wait(v, "vv")
    inc(v.tensor_copy(out=T.olf[:, 0:2], in_=T.oli[:, 0:2]), "vv")
    wait(v, "vv")
    wait(v, "ci")
    for k in range(2):
        inc(v.tensor_scalar(out=T.eh[:, 8 + 8 * k:16 + 8 * k], in0=T.io16b[:, 0:8], scalar1=T.olf[:, k:k + 1], scalar2=None,
                            op0=A.is_equal), "vt")
    wait(pe, "ca")
    wait(pe, "vt")
    pe.matmul(T.pc[:, 0:16], T.upd[:, :], T.eh[:, 8:24], False, False)
    inc(pe.matmul(T.pc[:, 0:16], T.onesb[:, :], T.eh[:, 0:16], False, True), "tv")
    inc(v.tensor_scalar(out=T.oli[:, 2:4], in0=T.ent[:, :], scalar1=R - 1, scalar2=None, op0=A.bitwise_and), "vv")
    wait(v, "vv")
    inc(v.tensor_scalar(out=T.olf[:, 2:4], in0=T.oli[:, 2:4], scalar1=-float(MID), scalar2=None, op0=A.add), "vv")
    wait(v, "tv")
    for k in range(2):
        inc(v.tensor_reduce(out=T.slotf[:, k:k + 1], in_=T.pc[:, 8 * k:8 * k + 8], axis=AxisListType.X, op=A.max), "sl")
    wait(sc, "sl")
    wait(sc, "cb")
    for k in range(2):
        inc(sc.activation(out=T.junk[:, QW * k:QW * k + QW], in_=T.cs2[:, :], func=AF.Sign, bias=T.slotf[:, k:k + 1], scale=-0.5,
                          accum_out=T.a2[:, k:k + 1]), "sa%d" % k)
    wait(v, "sl")
    inc(v.tensor_scalar(out=T.sl8[:, :], in0=T.slotf[:, :], scalar1=0.125, scalar2=-float(BIG // 8 + QW), op0=A.mult, op1=A.add),
        "vv")
    wait(v, "vv")
    wait(v, "cb")
    wait(v, "c8")

    last = None
    for k in range(2):
        lq = T.lq[:, 128 * k:128 * k + 128]
        rq = T.rq[:, QW * k:QW * k + QW]
        wait(v, "sa%d" % k)
        inc(v.tensor_scalar(out=lq, in0=T.m8b[:, :], scalar1=T.a2[:, k:k + 1], scalar2=T.sl8[:, k:k + 1],
                            op0=A.add, op1=A.is_equal), "vq%d" % k)
        inc(v.tensor_scalar(out=rq, in0=T.c2b[:, :], scalar1=T.a2[:, k:k + 1], scalar2=T.olf[:, 2 + k:3 + k],
                            op0=A.is_equal, op1=A.mult), "vq%d" % k)
        wait(pe, "vq%d" % k)
        last = pe.matmul(T.pq[:, 0:QW], lq, rq, k == 0, k == 1)
    inc(last, "tv")
    wait(v, "tv")
    inc(v.tensor_scalar(out=T.qm[:, :], in0=T.pq[:, 0:QW], scalar1=float(MID), scalar2=None, op0=A.add), "qs")

    here = T.qin[:, 8 * me:8 * me + BW]
    left = 0
    wait(g, "qs")
    for i, stage in enumerate(stages + [[(nearc, enear)]]):
        g.remote_dma_fused([
            RemoteDMATransfer(dst_ids=[dst(d)], dma_engine_mask=_mask(eng), remote_sem=T.sem["req%d" % i],
                              srcs=[T.qm[:, BW * T.rank_of(d):BW * T.rank_of(d) + BW]], dsts=[here])
            for d, eng in stage], local_sem=T.sem.loc)
        left += sum(len(eng) for d, eng in stage)

    wait(v, "cc")
    inc(v.tensor_scalar(out=T.ai[:, :], in0=T.ai[:, :], scalar1=3, scalar2=None, op0=A.arith_shift_right), "vv")
    inc(v.tensor_scalar(out=T.bi[:, :], in0=T.bi[:, :], scalar1=15, scalar2=None, op0=A.bitwise_and), "vv")
    wait(v, "vv")
    inc(v.tensor_scalar(out=T.af[:, :], in0=T.ai[:, :], scalar1=16, scalar2=None, op0=A.is_equal), "vv")
    inc(v.tensor_scalar(out=T.bf[:, :], in0=T.bi[:, :], scalar1=0, scalar2=None, op0=A.is_equal), "vv")
    wait(v, "vv")
    for k in range(2):
        inc(v.tensor_scalar(out=T.lf[:, 128 * k:128 * k + 128], in0=T.af[:, :], scalar1=T.slotf[:, k:k + 1], scalar2=None,
                            op0=A.mult), "vt")
    wait(pe, "vt")
    pe.matmul(T.pf[:, 0:16], T.lf[:, 0:128], T.bf[:, 0:16], True, False)
    inc(pe.matmul(T.pf[:, 0:16], T.lf[:, 128:256], T.bf[:, 16:32], False, True), "tv")
    wait(v, "tv")
    inc(v.tensor_scalar(out=T.fin[:, :], in0=T.pf[:, 0:16], scalar1=-float(BIG), scalar2=None, op0=A.add), "fs")

    def vpick(out, win, offs):
        return v.tensor_copy(out=out, in_=win.indirect(offs))

    def spick(out, win, offs):
        return sc.activation(out=out, in_=win.indirect(offs), func=AF.Copy)

    def asked(d, a=0, b=BW):
        q = T.rank_of(d)
        return T.snd[:, CAP * q + 16 * a:CAP * q + 16 * b], T.tabs[:, 0:R], T.qin[:, 8 * q + a:8 * q + b]

    wait(v, "ldt")
    wait(sc, "ldt")
    block = T.land[:, CAP * me:CAP * me + CAP]
    for i, stage in enumerate(stages):
        v.wait_ge(T.sem["req%d" % i], arrive[i])
        sc.wait_ge(T.sem["req%d" % i], arrive[i])
        inc(vpick(*asked(stage[0][0])), "gs%d" % i)
        inc(spick(*asked(stage[1][0])), "gs%d" % i)
        call = list(stage)
        if i == NS - 1:
            v.wait_ge(T.sem["req%d" % NS], arrive[NS])
            sc.wait_ge(T.sem["req%d" % NS], arrive[NS])
            inc(vpick(*asked(nearc, 0, BW // 2)), "gs%d" % i)
            inc(spick(*asked(nearc, BW // 2, BW)), "gs%d" % i)
            call.append((nearc, enear))
        wait(g, "gs%d" % i)
        g.remote_dma_fused([
            RemoteDMATransfer(dst_ids=[dst(d)], dma_engine_mask=_mask(eng), remote_sem=T.sem.dat,
                              srcs=[T.snd[:, CAP * T.rank_of(d):CAP * T.rank_of(d) + CAP]], dsts=[block])
            for d, eng in call], local_sem=T.sem.loc)
        left += sum(len(eng) for d, eng in call)
    wait(v, "qs")
    inc(vpick(block, T.tabs[:, 0:R], T.qm[:, BW * me:BW * me + BW]), "own")

    got = sum(arrive)
    for q, pick, h in ((v, vpick, 0), (sc, spick, 1)):
        q.wait_ge(T.sem.dat, got)
        wait(q, "own")
        wait(q, "fs")
        inc(pick(T.ysb[:, 128 * h:128 * h + 128], T.land[:, 0:N * CAP], T.fin[:, 8 * h:8 * h + 8]), "done")
    wait(sy, "done")
    inc(sy.dma_start(out=T.y[:, :], in_=T.ysb[:, :]), "st", 16)
    g.wait_ge(T.sem.loc, left)
    wait(g, "st")
